import numpy as np, ml_dtypes
CORES = [36,164,52,180,100,228,116,244]
N = 8
BF = ml_dtypes.bfloat16
def gentries(a):
    return np.ascontiguousarray(a.reshape(8, 16, -1).transpose(0, 2, 1)).reshape(8, -1)
def gtable(e):
    e = np.asarray(e); return np.ascontiguousarray(e.reshape(8, -1, 16).transpose(0, 2, 1)).reshape(128, -1).astype(np.int32)
S, A, DB, RO, MX = 1536, 3, 4, 3, 15
U = 128 >> DB
def parts(rng):
    nx = rng.integers(0, S, (N, 8, A, S))
    nx[:, 1::3] = (np.arange(S) + rng.integers(1, S // 8, nx[:, 1::3].shape)) % S
    lev = rng.random((N, 8, 16, 1), dtype=np.float32) * np.float32(0.75) + np.float32(0.25)
    rw = np.minimum(np.floor(rng.random((N, 8, 16, A * S), dtype=np.float32) * lev * np.float32(MX + 1)), np.float32(MX))
    cap = rng.integers(MX + 1, 129, (N, 8, 16, 1)); act = rng.integers(0, A, (N, 8, S))
    return nx, rw, cap, act
def pack(nx, rw, cap, act):
    return {"nx": np.stack([gtable(a.reshape(8, -1)) for a in nx]), "rw": np.ascontiguousarray(rw).reshape(N, 128, A * S).astype(np.float32).astype(BF),
            "cap": np.ascontiguousarray(cap).reshape(N, 128, 1).astype(np.float32), "act0": np.stack([gtable(a) for a in act])}
def stage(rng, nx, rw, cap, g, to, rew):
    cap[:, g] = 128
    for p in range(N):
        z, e, f = [int(v) for v in rng.permutation(S)[:3]]
        nx[p, g] = np.array([z, e, f])[to[p]]
        nx[p, g, :, z] = z; nx[p, g, :, e] = f; nx[p, g, :, f] = f
        rew[p, :, :, z] = 0; rew[p, :, :, e] = 0; rew[p, :, :, f] = U
    rw[:, g] = rew.reshape(N, 16, A * S)
def swing(rng):
    to = np.where(rng.random(S) < 0.4, 2 * rng.integers(0, 2, (1, A, S)), rng.integers(0, 3, (N, A, S)))
    rew = rng.integers(0, MX + 1, (N, 16, A, S)) * (rng.random(S) < 0.5)
    return to, rew
def brim(rng):
    to = 1 + (rng.random((N, A, S)) < 0.3).astype(np.int64)
    short = rng.random((N, 16, A, S)) * (16 * N) < 1
    return to, np.where(short, U - 1, rng.integers(U, MX + 1, short.shape))
def tug(rng):
    h = N // 2; o = rng.permutation(N); p, q = o[:h], o[h:2 * h]
    low = rng.integers(0, U + 1, (h, 16, A, S)) * (rng.random(S) < 0.7)
    high = U - low.reshape(16 * h, A, S)[rng.permutation(16 * h)].reshape(low.shape)
    b = rng.random((h, A, S)) < 0.5
    to = np.zeros((N, A, S), np.int64); rew = np.zeros((N, 16, A, S), np.int64)
    to[p] = np.where(b, 1, 0); to[q] = np.where(b, 0, 1)
    rew[p] = np.where(b[:, None], high, low); rew[q] = np.where(b[:, None], low, high)
    x = rng.random(rew.shape) * (16 * N)
    rew = rew + (x < 0.5).astype(np.int64) - (x > 16 * N - 0.5).astype(np.int64)
    return to, np.minimum(np.maximum(rew, 0), MX)
def setup_inputs(rng):
    return pack(*parts(rng))
def setup_inputs_ties(rng):
    nx, rw, cap, act = parts(rng); w = rw.reshape(N, 8, 16, A, S)
    nx[:, 0::4, 1:] = nx[:, 0::4, :1]; w[:, 0::4, :, 1:] = w[:, 0::4, :, :1]
    for g in (1, 5):
        m = rng.random(S) < 0.5
        nx[:, g] = np.where(m, nx[:, g, :1], nx[:, g]); w[:, g] = np.where(m, w[:, g, :, :1], w[:, g])
    for g in (2, 6):
        nx[:, g, 1:] = nx[:, g, :1]; cap[:, g] = 128
        w[:, g] = (4 * (rng.random((N, 16, 1, S)) < 0.3)).astype(np.float32)
        q = int(rng.integers(0, N)); i = int(rng.integers(0, 16))
        w[q, g, i] = 1; w[q, g, i, A - 1] = rng.integers(0, 3, S)
    for g in (3, 7):
        w[:, g] = MX * (rng.random((N, 16, A, S)) < 0.3).astype(np.float32); cap[:, g] = MX + 1
    return pack(nx, w, cap, act)
def setup_inputs_full(rng):
    nx, rw, cap, act = parts(rng)
    v = rng.integers(1, MX + 1, (N, 8, 16, 1))
    rw = np.where(rng.random(rw.shape, dtype=np.float32) < 0.03, rw, v.astype(np.float32))
    near = v * 2 ** DB + rng.integers(-1, 2, v.shape); ends = rng.choice(np.array([MX + 1, MX + 2, 127, 128]), v.shape)
    cap = np.minimum(np.maximum(np.where(rng.random(v.shape) < 0.6, near, ends), MX + 1), 128)
    rw[:, 0] = MX; rw[:, 1] = np.where(rng.random(rw[:, 1].shape) < 0.01, 1 + rng.integers(0, MX, rw[:, 1].shape), 0)
    return pack(nx, rw, cap, act)
def setup_inputs_chains(rng):
    nx, rw, cap, act = parts(rng); s = np.arange(S); a = np.arange(A)[:, None]
    nx[:, 0] = s; nx[:, 1] = np.minimum(s + 1 + a, S - 1); nx[:, 2] = (s - 1 - a) % S
    nx[:, 3] = rng.integers(0, S, (N, A, 1)); nx[:, 4] = np.argsort(rng.random((N, A, S)), axis=-1)
    nx[:, 5] = (S - 1) * rng.integers(0, 2, (N, A, S)); nx[:, 6, ::2] = s ^ 1; nx[:, 7] = nx[:1, 7]
    act[:, 1] = 0; act[:, 2] = A - 1; act[:, 4] = act[:1, 4]
    return pack(nx, rw, cap, act)
def setup_inputs_loud(rng):
    nx, rw, cap, act = parts(rng); o = rng.permutation(N); big = np.zeros((N, 8, 1, 1), bool)
    for g in range(8): big[o[g % N], g] = True
    big[:, 2] = True
    rw = np.where(big | (rng.random(rw.shape, dtype=np.float32) < 0.01), rw, np.float32(0))
    rw[o[0], 2] = 0; rw[:, 3] = 0
    for p in range(N):
        if not big[p, 7, 0, 0]: rw[p, 7] = 0
    for g, make in ((1, swing), (5, brim), (6, tug)):
        to, rew = make(rng); stage(rng, nx, rw, cap, g, to, rew)
    return pack(nx, rw, cap, act)
def setup_inputs_spread(rng):
    nx, rw, cap, act = parts(rng)
    e = np.exp2(rng.integers(-2, 3, (N, 8, 16, 1)) + rng.integers(-2, 3, (N, 8, 1, A * S))).astype(np.float32)
    rw = np.minimum(np.floor(np.float32(MX + 1) * rng.random(rw.shape, dtype=np.float32) ** e), np.float32(MX))
    nx = np.minimum(np.floor(S * rng.random(nx.shape) ** np.exp2(rng.integers(-2, 3, (N, 8, 1, 1)))).astype(np.int64), S - 1)
    cap = np.minimum(np.floor((MX + 1) * np.exp2(rng.random(cap.shape) * np.log2(128 / (MX + 1)) * 1.02)).astype(np.int64), 128)
    act = np.minimum(np.floor(A * rng.random(act.shape) ** 3).astype(np.int64), A - 1)
    return pack(nx, rw, cap, act)
def check_inputs(d):
    bad = []
    for k, lo, hi in (("nx", 0, S - 1), ("rw", 0, MX), ("cap", MX + 1, 128), ("act0", 0, A - 1)):
        v = np.asarray(d[k]).astype(np.float32)
        if not np.all((v >= lo) & (v <= hi) & (v == np.floor(v))): bad.append("range of " + k)
    return bad
def reference(nx, rw, cap, act0):
    n = np.stack([gentries(a) for a in nx]).astype(np.int64).reshape(N, 8, A, S)
    w = rw.astype(np.float32).astype(np.int32).reshape(N, 8, 16, A, S); c = cap.astype(np.int32).reshape(N, 8, 16, 1)
    act = np.stack([gentries(a) for a in act0]).astype(np.int64)
    for rnd in range(RO):
        t = np.take_along_axis(n, act[:, :, None, :], 2)[:, :, 0]
        r = np.take_along_axis(w, act[:, :, None, None, :], 3)[:, :, :, 0]
        for k in range(DB):
            r = np.minimum(r + np.take_along_axis(r, t[:, :, None, :], 3), c)
            t = np.take_along_axis(t, t, 2)
        q = np.zeros((8, A, S), np.int64)
        for p in range(N):
            for a in range(A):
                v = w[p][:, :, a] + np.take_along_axis(r[p], n[p][:, a][:, None, :], 2)
                q[:, a] += np.add.reduce(np.minimum(v, c[p]), axis=1)
        best = np.argmax(q, axis=1)
        act = np.stack([best for p in range(N)])
    return {"yr": r.reshape(N, 128, S).astype(np.float32).astype(BF), "ya": np.stack([gtable(a) for a in act]).astype(np.float32)}

from concourse.bass import DstId, RemoteDMATransfer
from concourse.mybir import AluOpType as A, ActivationFunctionType as F

NR, ROUNDS = 8, 3
S, NA = 1536, 3
M = S // 16
NV = 1152
NS = S - NV
MV, MS = NV // 16, NS // 16
TV = (0, 256, 256)
TF = (768, 896, 896)
RS = 1152
RC = (1024, 1024, RS)

_B, _H, _F = "bfloat16", "float16", "float32"
SCRATCH = {
    "nxi": ("sbuf", [128, 288], "int32"), "acti": ("sbuf", [128, 96], "int32"), "capf": ("sbuf", [128, 1], _F),
    "rwb": ("sbuf", [128, 4608], _B), "db": ("sbuf", [128, 3 * NV], _B), "xd": ("sbuf", [128, 4608], _B),
    "nx16": ("sbuf", [128, 288], _H), "nxu": ("sbuf", [128, 288], "uint16"), "dn": ("sbuf", [128, 192], _H),
    "xt": ("sbuf", [128, 576], "int32"), "xs": ("sbuf", [128, 576], "int32"), "xb": ("sbuf", [128, 576], _B),
    "lu": ("sbuf", [128, 96], "uint16"), "tu0": ("sbuf", [128, 96], "uint16"), "tu1": ("sbuf", [128, 96], "uint16"),
    "sti": ("sbuf", [128, 96], "int32"), "pi": ("sbuf", [128, 1], "int32"), "pm": ("sbuf", [128, 1], "int32"),
    "pf": ("sbuf", [128, 1], _F), "st16": ("sbuf", [128, 96], _H),
    "bb": ("sbuf", [128, 192], _H), "pr": ("sbuf", [128, 192], _H), "wm": ("sbuf", [128, 192], _F),
    "ra": ("sbuf", [128, S], _B), "rb": ("sbuf", [128, S], _B), "ta": ("sbuf", [128, S], _B), "tb": ("sbuf", [128, S], _B),
    "rk": ("sbuf", [128, S], _B), "zr": ("sbuf", [128, S - RS], _B),
    "tv0": ("sbuf", [128, NV], _B), "tv1": ("sbuf", [128, NV], _B), "tv2": ("sbuf", [128, NV], _B),
    "zs": ("sbuf", [128, 3 * NS], _B), "ts": ("sbuf", [128, 3 * NS], _B),
    "x0": ("sbuf", [128, MV], _F), "xs0": ("sbuf", [128, MS], _F),
    "eo": ("sbuf", [128, 2 * MV], _H), "eg": ("sbuf", [128, 192], _H),
    "yb": ("sbuf", [128, S], _B), "yt": ("sbuf", [128, 96], _F), "yf": ("sbuf", [128, 96], _F),
    "selx": ("sbuf", [128, 1024], _B), "pa": ("sbuf", [128, 128], _B), "pb": ("sbuf", [128, 128], _B),
    "idb": ("sbuf", [128, 128], _B), "i1": ("sbuf", [128, 128], _B), "i2": ("sbuf", [128, 128], _B),
    "zx": ("sbuf", [128, 144], _B), "zq": ("sbuf", [128, 144], _B), "nzq": ("sbuf", [128, 144], _B),
}
for _k in range(8):
    SCRATCH["b%d" % _k] = ("psum", [128, 512], _F)
    SCRATCH["ev%d" % _k] = ("sbuf", [128, 2 * MV], _H)
for _r in range(ROUNDS):
    SCRATCH["o%d" % _r] = ("sbuf", [128, 192], _H)
    for _k in range(NR):
        SCRATCH["v%d_%d" % (_r, _k)] = ("sbuf", [128, 192], _H)
SEMAPHORES = ["cV", "cS", "cP", "cG", "lnx", "lact", "lcap", "lrw0", "lrw1", "lrw2", "st0", "st1", "loc"]
SEMAPHORES += ["ae%d" % k for k in range(NR)] + ["a%d_%d" % (r, k) for r in range(ROUNDS) for k in range(NR)]


def rank_program(g, core, T, topo):
    rank = T.rank_of(core)
    if rank is None:
        return
    queue = {"V": g.vector, "S": g.scalar, "P": g.tensor, "G": g, "Y": g.sync}
    V, SC, PE = g.vector, g.scalar, g.tensor
    count = {"V": 0, "S": 0, "P": 0, "G": 0}
    seen = {}

    def wait(q, *toks):
        for name, val in toks:
            if seen.get((q, name), 0) < val:
                queue[q].wait_ge(T.sem[name], val)
                seen[(q, name)] = val

    def mark(q, ins):
        count[q] += 1
        ins.then_inc(T.sem["c" + q], 1)
        return ("c" + q, count[q])

    def load(q, name, out, in_):
        queue[q].dma_start(out, in_).then_inc(T.sem[name], 16)
        return (name, 16)

    def copy(deps, out, in_):
        wait("V", *deps)
        return mark("V", V.tensor_copy(out, in_))

    def tt(deps, out, a, b, op):
        wait("V", *deps)
        return mark("V", V.tensor_tensor(out, a, b, op))

    def tsc(deps, out, a, s1, s2, op0, op1=None):
        wait("V", *deps)
        if op1 is None:
            return mark("V", V.tensor_scalar(out, a, s1, None, op0))
        return mark("V", V.tensor_scalar(out, a, s1, s2, op0, op1))

    def act(deps, out, in_, func=F.Copy, *more):
        wait("S", *deps)
        return mark("S", SC.activation(out, in_, func, *more))

    def mm(deps, out, lhsT, rhs, start, stop):
        wait("P", *deps)
        ins = PE.matmul(out, lhsT, rhs, start, stop)
        return mark("P", ins) if stop else None

    def group(deps, out, pairs):
        wait("P", *deps)
        tok = None
        for n, (l, r) in enumerate(pairs):
            tok = mm([], out, l, r, n == 0, n == len(pairs) - 1)
        return tok

    def fold(deps, out, z, buf, a, b):
        return group(deps, out, [(z[:, 15 - i:143 - i], buf[:, a + i:b:16]) for i in range(16)])

    def select(tok, name, pattern, op, fill, base, cm):
        wait("G", tok)
        return mark("G", g.affine_select(T[name][:], T[name][:], pattern, op, fill, base, cm))

    tnx = load("Y", "lnx", T.nxi[:], T.nx[:])
    tact = load("S", "lact", T.acti[:], T.act0[:])
    tcap = load("S", "lcap", T.capf[:], T.cap[:])
    trw = [load("Y", "lrw%d" % a, T.rwb[:, a * S:(a + 1) * S], T.rw[:, a * S:(a + 1) * S]) for a in range(NA)]

    zero = {}
    for n in ("pa", "pb", "selx", "idb", "zx", "eg"):
        zero[n] = mark("V", V.memset(T[n][:], 0.0))
    zero["zq"] = mark("V", V.memset(T.zq[:], 1.0))
    pp = [[-16, 8], [1000, 2], [-1, 8]]
    k = select(zero["pa"], "pa", pp, A.not_equal, 256.0, 0, 1)
    kpa = select(k, "pa", pp, A.not_equal, 1.0, -1000, 1)
    k = select(zero["pb"], "pb", pp, A.not_equal, 256.0, -8, 1)
    kpb = select(k, "pb", pp, A.not_equal, 1.0, -1008, 1)
    ksx = select(zero["selx"], "selx", [[-1, 8], [-8, 16], [0, 8]], A.not_equal, 1.0, 0, 1)
    kid = select(zero["idb"], "idb", [[-1, 128]], A.not_equal, 1.0, 0, 1)
    ksti = mark("G", g.iota(T.sti[:], [[16, 96]], 0, 0))
    kpi = mark("G", g.iota(T.pi[:], [[1, 1]], 0, 1))
    k = select(zero["zx"], "zx", [[-16, 9], [1000, 16]], A.not_equal, 1.0, -15000, 1)
    kzx = select(k, "zx", [[-16, 9], [1000, 16]], A.not_equal, 256.0, -15008, 1)
    k = select(zero["zq"], "zq", [[0, 9], [1, 16]], A.is_ge, 0.0, -15, 0)
    k = select(k, "zq", [[-16, 9], [0, 16]], A.is_ge, 0.0, 0, 1)
    kzq = select(k, "zq", [[16, 9], [0, 16]], A.is_ge, 0.0, 15, -1)

    t16 = copy([tnx], T.nx16[:], T.nxi[:])
    pA = group([t16, kpa], T.b1[:, 0:288], [(T.pa[:], T.nx16[:])])
    pB = group([kpb], T.b2[:, 0:288], [(T.pb[:], T.nx16[:])])
    b1t = tsc([tact], T.bb[:, 0:96], T.acti[:], 1.0, None, A.is_equal)
    b2t = tsc([], T.bb[:, 96:192], T.acti[:], 2.0, None, A.is_equal)

    def digits(p, bank, lo):
        c = slice(lo, lo + 288)
        a = copy([p], T.xt[:, c], bank[:, 0:288])
        b = tsc([a], T.xs[:, c], T.xt[:, c], 8, 255, A.logical_shift_right, A.bitwise_and)
        return copy([b], T.xb[:, c], T.xs[:, c])

    dig = [digits(pA, T.b1, 0), digits(pB, T.b2, 288)]
    kdn = [tt([t16], T.dn[:, 96 * a:96 * a + 96], T.nx16[:, 96 * a + 96:96 * a + 192], T.nx16[:, 0:96], A.subtract)
           for a in range(2)]
    ki1 = tsc([kid], T.i1[:], T.idb[:], 1536.0, None, A.mult)
    ki2 = tsc([], T.i2[:], T.idb[:], 3072.0, None, A.mult)
    kpm = tsc([kpi], T.pm[:], T.pi[:], 15, None, A.bitwise_and)
    kpf = copy([kpm], T.pf[:], T.pm[:])
    kst = tsc([kpf, ksti], T.st16[:], T.sti[:], T.pf[:], None, A.add)
    kn0 = copy([], T.nxu[:], T.nxi[:])
    bank_free = {}
    xdt = []
    for n in range(16):
        h, j = n // 8, n % 8
        b = 3 + n % 5
        src = T["b%d" % b][:, 0:288]
        tok = group([ksx, dig[h]] + bank_free.get(b, []), src,
                    [(T.selx[:, 128 * j:128 * j + 128], T.xb[:, 288 * h:288 * h + 288])])
        out = T.xd[:, j + 8 * h::16]
        if h == 0 or j % 2 == 1:
            bank_free[b] = [act([tok], out, src)]
        else:
            bank_free[b] = [copy([tok], out, src)]
        xdt += bank_free[b]

    def caps(q, a):
        out, in_ = T.db[:, a * NV:a * NV + NV], T.rwb[:, a * S:a * S + NV]
        wait(q, trw[a], tcap)
        if q == "V":
            return mark("V", V.tensor_scalar(out, in_, -1.0, T.capf[:], A.mult, A.add))
        return mark("S", SC.activation(out, in_, F.Identity, T.capf[:], -1.0))

    T_, R_, TU = [T.ta, T.tb], [T.ra, T.rb], [T.tu0, T.tu1]
    others = [T.cores[(rank + n) % NR] for n in range(1, NR)]
    before = [(rank - n) % NR for n in range(1, NR)]

    def share(deps, src, land, sem):
        wait("G", *deps)
        mask = topo.mask(core, others[0])
        ids = []
        for d in others:
            mask &= topo.mask(core, d)
            rid, pid = topo.addr(d, core)
            ids.append(DstId(rid=rid, pnc=pid))
        g.remote_dma_fused([RemoteDMATransfer(dst_ids=ids, dma_engine_mask=mask, remote_sem=T.sem[sem], srcs=[src],
                                              dsts=[land for d in others])], local_sem=T.sem["loc"])
        return len([n for n in range(16) if mask >> n & 1])

    sent = 0
    tb_ = [b1t, b2t] + bank_free[5]
    for rnd in range(ROUNDS):
        first, last = rnd == 0, rnd == ROUNDS - 1
        pL = group(tb_ + [ki1, ki2, kst], T.b5[:, 0:96],
                   [(T.i1[:], T.bb[:, 0:96]), (T.i2[:], T.bb[:, 96:192]), (T.idb[:], T.st16[:])])
        kpr = tt(tb_ + kdn, T.pr[:], T.bb[:], T.dn[:], A.mult)
        kl = copy([pL], T.lu[:], T.b5[:, 0:96])
        pT = group([kpr], T.b0[:, 0:96], [(T.idb[:], T.nx16[:, 0:96]), (T.idb[:], T.pr[:, 0:96]), (T.idb[:], T.pr[:, 96:192])])
        kt = act([kl] + (xdt if first else []), T.ta[:], T.xd[:].indirect(T.lu[:]))
        if first:
            kd = [caps("V", 0), None, caps("V", 2)]
        wait("V", kl, *trw)
        kr = [copy([], T.ra[:, 0:RC[0]], T.rwb[:].indirect(T.lu[:, 0:RC[0] // 16]))]
        ktu = copy([pT], T.tu0[:], T.b0[:, 0:96])
        kr.append(copy([], T.ra[:, RC[0]:S], T.rwb[:].indirect(T.lu[:, RC[0] // 16:M])))
        krk = [copy(kr, T.rk[:], T.ra[:])]
        if first:
            knz = tsc([kzq], T.nzq[:], T.zq[:], -1.0, None, A.mult)
            pe = [fold([trw[a], kzq] + xdt, T["b%d" % (1 + a)][:, 0:MV], T.zq, T.rwb, a * S, a * S + NV) for a in range(NA)]

        def preload():
            for a in range(NA):
                mm([kid], T["b%d" % (1 + a)][:, 0:NS], T.idb[:], T.rwb[:, a * S + NV:a * S + S], True, False)

        if not first:
            preload()
        cur = 0
        ktx = [kt]
        for st in range(3):
            tc, tn, rc, rn, tu, tun = T_[cur], T_[1 - cur], R_[cur], R_[1 - cur], TU[cur], TU[1 - cur]
            tv, tf, rcut = TV[st], TF[st], RC[st]
            hv = [copy([ktu] + ktx, tn[:, 0:tv], tc[:].indirect(tu[:, 0:tv // 16]))] if tv else []
            h1 = act([ktu] + ktx, tn[:, tv:tf], tc[:].indirect(tu[:, tv // 16:tf // 16]))
            h2 = act([], tn[:, tf:S], tc[:].indirect(tu[:, tf // 16:M]))
            ktx = hv + [h2]
            fold(hv + [h1, kzx], T.b0[:, 0:tf // 16], T.zx, tn, 0, tf)
            px = fold([h2], T.b0[:, tf // 16:M], T.zx, tn, tf, S)
            k1 = tt(kr + krk + [ktu], rn[:, 0:rcut], rc[:].indirect(tu[:, 0:rcut // 16]), T.rk[:, 0:rcut], A.add)
            k2 = tt([], rn[:, rcut:S], rc[:].indirect(tu[:, rcut // 16:M]), T.rk[:, rcut:S], A.add)
            kr = [k2]
            krk = [act([k1], T.rk[:, 0:rcut], rn[:, 0:rcut])]
            if st < 2:
                krk.append(copy([k2], T.rk[:, rcut:S], rn[:, rcut:S]))
            if first and st == 0:
                k = copy([pe[0]], T.x0[:], T.b1[:, 0:MV])
                tt([k, pe[1]], T.eo[:, 0:MV], T.b2[:, 0:MV], T.x0[:], A.subtract)
                ke = tt([pe[2]], T.eo[:, MV:2 * MV], T.b3[:, 0:MV], T.x0[:], A.subtract)
                sent += share([ke], T.eo[:], T["ev%d" % rank][:], "ae%d" % rank)
            ktu = copy([px], tun[:], T.b0[:, 0:96])
            cur = 1 - cur
        rc, rn, tu = R_[cur], R_[1 - cur], TU[cur]
        mm(kr, T.b6[:, 0:S - RS], T.idb[:], rc[:, RS:S], True, False)
        hz = act([ktu] + kr, T.zr[:], rc[:].indirect(tu[:, RS // 16:M]))
        pz = mm([hz], T.b6[:, 0:S - RS], T.idb[:], T.zr[:], False, True)
        ks = act([pz], rn[:, RS:S], T.b6[:, 0:S - RS])
        kv = tt([ktu] + kr + krk, rn[:, 0:RS], rc[:].indirect(tu[:, 0:RS // 16]), T.rk[:, 0:RS], A.add)
        if first:
            wait("P", ke)
            preload()
            kd[1] = caps("S", 1)
        hz = [act([kv, ks, kn0], T.zs[:, a * NS:a * NS + NS], rn[:].indirect(T.nxu[:, a * M + MV:a * M + M])) for a in range(NA)]
        pz = [mm([hz[a]], T["b%d" % (1 + a)][:, 0:NS], T.idb[:], T.zs[:, a * NS:a * NS + NS], False, True) for a in range(NA)]
        wait("S", tcap)
        kre = [act([pz[a]], T.ts[:, a * NS:a * NS + NS], T["b%d" % (1 + a)][:, 0:NS], F.Relu, T.capf[:], -1.0) for a in range(NA)]
        hv = [tt([kv, ks, kd[a]], T["tv%d" % a][:], rn[:].indirect(T.nxu[:, a * M:a * M + MV]), T.db[:, a * NV:a * NV + NV], A.min)
              for a in range(NA)]
        pv0 = fold([hv[0], kzq], T.b4[:, 0:MV], T.zq, T.tv0, 0, NV)
        if first:
            pv1 = fold([hv[1]], T.b5[:, 0:MV], T.zq, T.tv1, 0, NV)
        ps = fold([kre[2], knz], T.b7[:, 0:3 * MS], T.nzq, T.ts, 0, 3 * NS)
        if not first:
            pv1 = fold([hv[1]], T.b5[:, 0:MV], T.zq, T.tv1, 0, NV)
        pv2 = fold([hv[2]], T.b6[:, 0:MV], T.zq, T.tv2, 0, NV)
        kx0 = act([pv0], T.x0[:], T.b4[:, 0:MV])
        kx1 = act([ps], T.xs0[:], T.b7[:, 0:MS])
        o = T["o%d" % rnd]
        tt([kx1], o[:, MV:M], T.b7[:, MS:2 * MS], T.xs0[:], A.subtract)
        tt([], o[:, M + MV:2 * M], T.b7[:, 2 * MS:3 * MS], T.xs0[:], A.subtract)
        tt([pv1, kx0], o[:, 0:MV], T.b5[:, 0:MV], T.x0[:], A.subtract)
        ko = tt([pv2], o[:, M:M + MV], T.b6[:, 0:MV], T.x0[:], A.subtract)
        sent += share([ko], o[:], T["v%d_%d" % (rnd, rank)][:], "a%d_%d" % (rnd, rank))
        if last:
            wait("V", tcap)
            ky = tsc([kv, ks], T.yb[:], rn[:], T.capf[:], None, A.min)
            wait("Y", ky)
            sy = load("Y", "st0", T.yr[:], T.yb[:])
        if first:
            mm([ke, ko], T.b7[:, 0:2 * MV], T.idb[:], T.eo[:], True, False)
            for n, p in enumerate(before):
                k = mm([("ae%d" % p, 8)], T.b7[:, 0:2 * MV], T.idb[:], T["ev%d" % p][:], False, n == NR - 2)
            copy([k], T.eg[:, 0:MV], T.b7[:, 0:MV])
            keg = copy([], T.eg[:, M:M + MV], T.b7[:, MV:2 * MV])
        mm([keg, ko], T.b4[:, 0:192], T.idb[:], T.eg[:], True, False)
        mm([], T.b4[:, 0:192], T.idb[:], o[:], False, False)
        for n, p in enumerate(before):
            pD = mm([("a%d_%d" % (rnd, p), 8)], T.b4[:, 0:192], T.idb[:], T["v%d_%d" % (rnd, p)][:], False, n == NR - 2)
        tsc([pD], T.wm[:, 0:96], T.b4[:, 96:192], -1.0, 0.0, A.add, A.max)
        kw = tsc([], T.wm[:, 96:192], T.b4[:, 0:96], 0.0, None, A.max)
        kb = tt([kw], T.bb[:], T.b4[:, 0:192], T.wm[:], A.is_gt)
        tb_ = [kb]
    k = tsc([kb], T.yt[:], T.bb[:, 96:192], 2.0, None, A.mult)
    k = tt([k], T.yf[:], T.yt[:], T.bb[:, 0:96], A.add)
    wait("Y", k)
    sa = load("Y", "st1", T.ya[:], T.yf[:])
    wait("Y", sy, sa)
    wait("G", ("loc", sent), ("cV", count["V"]), ("cS", count["S"]), ("cP", count["P"]), ("cG", count["G"]))
